import numpy as np
import ml_dtypes


def mxq(x, axis, fmt="e4m3"):
    dtype, down = {"e4m3": (ml_dtypes.float8_e4m3fn, 7), "e5m2": (ml_dtypes.float8_e5m2, 14)}[fmt]
    v = np.moveaxis(np.asarray(x, np.float32).astype(ml_dtypes.bfloat16).astype(np.float64), axis, -1)
    blocks = v.reshape(v.shape[:-1] + (-1, 32))
    amax = np.abs(blocks).max(-1, keepdims=True)
    byte = np.maximum(np.where(amax > 0, np.frexp(amax)[1] - 1 + 127, 0) - down, 1)
    scale = np.exp2(byte - 127.0)
    codes = (blocks / scale).astype(np.float32).astype(dtype).astype(np.float64)
    return np.moveaxis((codes * scale).reshape(v.shape), -1, axis)


WIDE = False


def mx_kscale(k):
    if not WIDE:
        return np.ones(k)
    levels = np.array([10, -10, 5, -5, 0])
    if k % 512:
        return np.exp2(np.random.permutation(np.resize(levels, k // 32))).repeat(32)
    a = np.empty((k // 512, 16))
    for p in range(k // 512):
        a[p, :8] = np.random.permutation(np.resize(levels, 8))
        for g in range(8):
            far = levels[np.abs(levels - a[p, g]) >= 10]
            a[p, g + 8] = far[np.random.randint(len(far))]
    return np.exp2(a.ravel()).repeat(32)


def f64(x):
    return np.asarray(x).astype(np.float64)


def striped(idx):
    return np.tile(idx.reshape(-1, 16).T, (8, 1)).astype(np.uint16)


def unstriped(offs):
    return offs[:16].T.reshape(-1).astype(np.int64)


K, T, E, C, N = 2560, 640, 20, 128, 128
TOP = 4


def by_expert(wq, xq):
    return np.concatenate([wq[e].T @ xq[:, e * C:(e + 1) * C] for e in range(E)], axis=1)


def setup_inputs():
    n = np.random.standard_normal
    s = mx_kscale(K)[:, None]
    deal = np.repeat(np.arange(E), C).reshape(TOP, T)[:, np.random.permutation(T)]
    deal = np.take_along_axis(deal, np.argsort(np.random.rand(TOP, T), axis=0), axis=0)
    for _ in range(8):
        s_, t_ = np.random.permutation(T).reshape(2, -1); r = np.random.randint(TOP, size=T // 2); x, y = deal[r, s_].copy(), deal[r, t_].copy()
        ok = ~((deal[:, s_] == y).any(0) | (deal[:, t_] == x).any(0)); deal[r[ok], s_[ok]] = y[ok]; deal[r[ok], t_[ok]] = x[ok]
    order = np.lexsort((np.random.rand(TOP * T), deal.reshape(-1)))
    slot_token = order % T; pos = np.empty(TOP * T, np.int64); pos[order] = np.arange(TOP * T); pos = pos.reshape(TOP, T)
    g = np.random.uniform(0.5, 1.5, (TOP, T)); g = g / g.sum(0)
    return {
        "xT": (n((K, T)) * s).astype(np.float32),
        "w": (n((E, K, N)) / np.sqrt(K) / s[None]).astype(np.float32),
        "gate": np.stack([np.tile(r, (N, 1)) for r in g]).astype(np.float32),
        "offs": striped(slot_token),
        "pos1": striped(pos[0]),
        "pos2": striped(pos[1]),
        "pos3": striped(pos[2]),
        "pos4": striped(pos[3]),
    }


def reference(xT, w, gate, offs, pos1, pos2, pos3, pos4):
    idx = unstriped(offs)
    xq = mxq(f64(xT)[:, idx], 0, "e4m3")
    y = by_expert(mxq(f64(w), 1, "e4m3"), xq)
    return sum(f64(gate[r]) * y[:, unstriped(p)] for r, p in enumerate((pos1, pos2, pos3, pos4)))

@@ -1,0 +1,179 @@
+from contextlib import ExitStack
+
+import concourse.mybir as mybir
+
+K, T, E, C, N = 2560, 640, 20, 128, 128
+SLOTS = E * C
+P = 128
+PASSES = 5
+UNITS = E * PASSES
+FLOPS = 2 * SLOTS * K * N
+
+F32 = mybir.dt.float32
+BF16 = mybir.dt.bfloat16
+U32 = mybir.dt.uint32
+U16 = mybir.dt.uint16
+U8 = mybir.dt.uint8
+FP8X4 = mybir.dt.float8_e4m3fn_x4
+MULT = mybir.AluOpType.mult
+
+GROUP = 3
+EARLY = 2
+CHUNKS = [4] * 24 + [2, 1, 1]
+BANK_EXPERTS = [[0, 1, 2, 3], [4, 5, 6, 7], [8, 9, 10, 11], [12, 13, 14, 15], [16, 17, 18], [19]]
+
+
+def tile_moe_tk_lin_none_kernel(tc, xT, w, gate, offs, pos1, pos2, pos3, pos4, out):
+    nc = tc.nc
+    with ExitStack() as ctx:
+        keep = ctx.enter_context(tc.tile_pool(name="keep", bufs=1))
+        xraw_pool = ctx.enter_context(tc.tile_pool(name="xraw", bufs=3))
+        xgrp_pool = ctx.enter_context(tc.tile_pool(name="xgrp", bufs=2))
+        wraw_pool = ctx.enter_context(tc.tile_pool(name="wraw", bufs=9))
+        group_pool = ctx.enter_context(tc.tile_pool(name="group", bufs=2))
+        wgrp_pool = ctx.enter_context(tc.tile_pool(name="wgrp", bufs=8))
+        wq_pool = ctx.enter_context(tc.tile_pool(name="wq", bufs=10))
+        psum = ctx.enter_context(tc.psum_pool(name="psum", bufs=1))
+
+        offs_t = keep.tile([P, SLOTS // 16], U16, name="offs_t")
+        nc.sync.dma_start(offs_t[:], offs)
+        pos_t = [keep.tile([P, T // 16], U16, name=f"pos_t{r}") for r in range(4)]
+
+        words = [keep.tile([P, T], U32, name=f"words{a}", align_bytes=64) for a in range(PASSES)]
+        bytes_a = keep.tile([P, T], U8, name="bytes_a", align_bytes=64)
+        bytes_b = keep.tile([P, T], U8, name="bytes_b", align_bytes=64)
+        gwords_early = [keep.tile([P, SLOTS], U32, name=f"gwords{a}", align_bytes=64) for a in range(EARLY)]
+        y = keep.tile([P, SLOTS], F32, name="y")
+        half = keep.tile([P, 2, T], F32, name="half")
+        res = keep.tile([P, T], F32, name="res")
+        banks = [psum.tile([P, 512], F32, name=f"bank{b}") for b in range(len(BANK_EXPERTS))]
+
+        nc.gpsimd.memset(bytes_a[:], 0)
+        nc.gpsimd.memset(bytes_b[:], 0)
+
+        def gather(dst, src, first, count):
+            nc.vector.tensor_copy(dst, src[:].indirect(offs_t[:, first // 16 : (first + count) // 16]))
+
+        for a in range(PASSES):
+            raw = xraw_pool.tile([P, 4, T], F32, name="xraw")
+            nc.sync.dma_start(raw[:], xT[512 * a : 512 * (a + 1), :].rearrange("(p j) t -> p j t", j=4))
+            grp = xgrp_pool.tile([P, T, 4], BF16, name="xgrp", align_bytes=64)
+            for lo, hi, eng in ((0, 256, "s"), (256, 640, "v")) if a == 0 else ((0, 640, "s"),):
+                dst = grp[:, lo:hi, :].rearrange("p (c i) t -> p c t i", i=4)
+                src = raw[:, :, lo:hi].rearrange("p t (c i) -> p c t i", i=4)
+                if eng == "s":
+                    nc.scalar.copy(dst, src)
+                else:
+                    nc.vector.tensor_copy(dst, src)
+            flat = grp[:].rearrange("p t j -> p (t j)")
+            plane, k = (bytes_a, 4 * a) if a < 4 else (bytes_b, 0)
+            for lo, hi in ((0, 512), (512, 640)):
+                nc.vector.quantize_mx(
+                    out=words[a][:, lo:hi].bitcast(FP8X4),
+                    scales=plane[k:P, lo:hi],
+                    in_=flat[:, 4 * lo : 4 * hi],
+                )
+            if a < EARLY:
+                for s in range(0, SLOTS, 480):
+                    c = min(480, SLOTS - s)
+                    gather(gwords_early[a][:, s : s + c], words[a], s, c)
+
+        w_units = w.rearrange("e (a p j) n -> p (e a) (j n)", a=PASSES, j=4)
+        bank_of = {e: (b, i) for b, es in enumerate(BANK_EXPERTS) for i, e in enumerate(es)}
+        firsts = [sum(CHUNKS[:i]) for i in range(len(CHUNKS))]
+        quantised = {}
+        groups = {}
+
+        def gather_group(g):
+            first = g * GROUP * C
+            count = min(GROUP * C, SLOTS - first)
+            late = []
+            for a in range(EARLY, PASSES):
+                t = group_pool.tile([P, GROUP * C], U32, name=f"late{a}", align_bytes=64)
+                gather(t[:, 0:count], words[a], first, count)
+                late.append(t)
+            ta = group_pool.tile([P, GROUP * C], U8, name="gba", align_bytes=64)
+            gather(ta[:, 0:count], bytes_a, first, count)
+            tb = group_pool.tile([P, GROUP * C], U8, name="gbb", align_bytes=64)
+            gather(tb[:, 0:count], bytes_b, first, count)
+            groups[g] = (late, ta, tb)
+
+        def interleave(eng, grp, raw, u0, u1, n0, n1):
+            dst = grp[:, u0:u1, n0:n1, :].rearrange("p u (c i) t -> p u c t i", i=4)
+            src = raw[:, u0:u1, :, n0:n1].rearrange("p u t (c i) -> p u c t i", i=4)
+            if eng == "s":
+                nc.scalar.copy(dst, src)
+            else:
+                nc.vector.tensor_copy(dst, src)
+
+        def prepare(ci):
+            unit, size = firsts[ci], CHUNKS[ci]
+            raw = wraw_pool.tile([P, 4, 4, N], F32, name="wraw")
+            nc.sync.dma_start(
+                raw[:, 0:size].rearrange("p u j n -> p u (j n)"), w_units[:, unit : unit + size, :]
+            )
+            grp = wgrp_pool.tile([P, 4, N, 4], BF16, name="wgrp", align_bytes=64)
+            if size < 4:
+                shares = (("s", 0, size, 0, N // 2), ("v", 0, size, N // 2, N))
+            else:
+                shares = (("s", 0, 4, 0, N),)
+            for eng, u0, u1, n0, n1 in shares:
+                interleave(eng, grp, raw, u0, u1, n0, n1)
+            codes = wq_pool.tile([P, 4 * N], U32, name="wcodes", align_bytes=64)
+            scales = wq_pool.tile([P, 4 * N], U8, name="wscales", align_bytes=64)
+            nc.vector.quantize_mx(
+                out=codes[:, 0 : size * N].bitcast(FP8X4),
+                scales=scales[:, 0 : size * N],
+                in_=grp[:, 0:size].rearrange("p u n j -> p (u n j)"),
+            )
+            quantised[ci] = (codes, scales)
+
+        def multiply(ci):
+            unit, size = firsts[ci], CHUNKS[ci]
+            codes, scales = quantised.pop(ci)
+            for u in range(size):
+                e, a = divmod(unit + u, PASSES)
+                b, i = bank_of[e]
+                g = e // GROUP
+                if g not in groups:
+                    gather_group(g)
+                late, ta, tb = groups[g]
+                here = slice((e - g * GROUP) * C, (e - g * GROUP + 1) * C)
+                plane, k = (ta, 4 * a) if a < 4 else (tb, 0)
+                rhs = gwords_early[a][:, e * C : (e + 1) * C] if a < EARLY else late[a - EARLY][:, here]
+                nc.tensor.matmul_mx(
+                    out=banks[b][:, i * C : (i + 1) * C],
+                    lhsT=codes[:, u * N : (u + 1) * N].bitcast(FP8X4),
+                    lhsT_scale=scales[:, u * N : (u + 1) * N],
+                    rhs=rhs.bitcast(FP8X4),
+                    rhs_scale=plane[k:P, here],
+                    start=(a == 0),
+                    stop=(a == PASSES - 1),
+                )
+                if a == PASSES - 1 and e == BANK_EXPERTS[b][-1]:
+                    first = BANK_EXPERTS[b][0] * C
+                    width = len(BANK_EXPERTS[b]) * C
+                    nc.scalar.copy(y[:, first : first + width], banks[b][:, 0:width])
+
+        LAG = 3
+        for ci in range(len(CHUNKS) + LAG):
+            if ci < len(CHUNKS):
+                prepare(ci)
+            if ci == 20:
+                for t, src in zip(pos_t, (pos1, pos2, pos3, pos4)):
+                    nc.sync.dma_start(t[:], src)
+            if ci == len(CHUNKS) - 1:
+                gate_t = xraw_pool.tile([P, 4, T], F32, name="xraw")
+                nc.sync.dma_start(gate_t[:], gate.rearrange("r p t -> p r t"))
+            if ci >= LAG:
+                multiply(ci - LAG)
+
+        prod = xraw_pool.tile([P, 4, T], F32, name="xraw")
+        for lo, hi in ((0, 320), (320, 640)):
+            for r in range(4):
+                nc.vector.tensor_tensor(
+                    prod[:, r, lo:hi], y[:].indirect(pos_t[r][:, lo // 16 : hi // 16]), gate_t[:, r, lo:hi], MULT
+                )
+            nc.vector.tensor_add(half[:, :, lo:hi], prod[:, 0:2, lo:hi], prod[:, 2:4, lo:hi])
+            nc.vector.tensor_add(res[:, lo:hi], half[:, 0, lo:hi], half[:, 1, lo:hi])
+            nc.sync.dma_start(out[:, lo:hi], res[:, lo:hi])

@@ -17,7 +17,10 @@ U8 = mybir.dt.uint8
 FP8X4 = mybir.dt.float8_e4m3fn_x4
 MULT = mybir.AluOpType.mult
 
-GROUP = 3
+GROUP = 2
+REGIONS = 9
+REGION = 4096
+AHEAD = 3
 EARLY = 2
 CHUNKS = [4] * 24 + [2, 1, 1]
 BANK_EXPERTS = [[0, 1, 2, 3], [4, 5, 6, 7], [8, 9, 10, 11], [12, 13, 14, 15], [16, 17, 18], [19]]
@@ -30,8 +33,7 @@ def tile_moe_tk_lin_none_kernel(tc, xT, w, gate, offs, pos1, pos2, pos3, pos4, o
         xraw_pool = ctx.enter_context(tc.tile_pool(name="xraw", bufs=3))
         xgrp_pool = ctx.enter_context(tc.tile_pool(name="xgrp", bufs=2))
         wraw_pool = ctx.enter_context(tc.tile_pool(name="wraw", bufs=9))
-        group_pool = ctx.enter_context(tc.tile_pool(name="group", bufs=2))
-        wgrp_pool = ctx.enter_context(tc.tile_pool(name="wgrp", bufs=8))
+        ring = ctx.enter_context(tc.tile_pool(name="ring", bufs=1))
         wq_pool = ctx.enter_context(tc.tile_pool(name="wq", bufs=10))
         psum = ctx.enter_context(tc.psum_pool(name="psum", bufs=1))
 
@@ -83,18 +85,24 @@ def tile_moe_tk_lin_none_kernel(tc, xT, w, gate, offs, pos1, pos2, pos3, pos4, o
         firsts = [sum(CHUNKS[:i]) for i in range(len(CHUNKS))]
         quantised = {}
         groups = {}
+        n_groups = (E + GROUP - 1) // GROUP
+        first_use = {g: g * GROUP * PASSES // 4 for g in range(n_groups)}
+        after = {first_use[g] - AHEAD: g for g in range(n_groups) if first_use[g] >= AHEAD}
+        region_of = {g: c % REGIONS for c, g in after.items()}
 
         def gather_group(g):
             first = g * GROUP * C
             count = min(GROUP * C, SLOTS - first)
+            at = (region_of[g] if g in region_of else REGIONS + g) * REGION
             late = []
             for a in range(EARLY, PASSES):
-                t = group_pool.tile([P, GROUP * C], U32, name=f"late{a}", align_bytes=64)
+                t = ring.tile([P, GROUP * C], U32, name=f"late{a}_{g}", align_bytes=64, offset=at)
+                at += 4 * GROUP * C
                 gather(t[:, 0:count], words[a], first, count)
                 late.append(t)
-            ta = group_pool.tile([P, GROUP * C], U8, name="gba", align_bytes=64)
+            ta = ring.tile([P, GROUP * C], U8, name=f"gba{g}", align_bytes=64, offset=at)
             gather(ta[:, 0:count], bytes_a, first, count)
-            tb = group_pool.tile([P, GROUP * C], U8, name="gbb", align_bytes=64)
+            tb = ring.tile([P, GROUP * C], U8, name=f"gbb{g}", align_bytes=64, offset=at + GROUP * C)
             gather(tb[:, 0:count], bytes_b, first, count)
             groups[g] = (late, ta, tb)
 
@@ -112,9 +120,11 @@ def tile_moe_tk_lin_none_kernel(tc, xT, w, gate, offs, pos1, pos2, pos3, pos4, o
             nc.sync.dma_start(
                 raw[:, 0:size].rearrange("p u j n -> p u (j n)"), w_units[:, unit : unit + size, :]
             )
-            grp = wgrp_pool.tile([P, 4, N, 4], BF16, name="wgrp", align_bytes=64)
+            grp = ring.tile([P, 4, N, 4], BF16, name=f"wgrp{ci}", align_bytes=64, offset=(ci % REGIONS) * REGION)
             if size < 4:
                 shares = (("s", 0, size, 0, N // 2), ("v", 0, size, N // 2, N))
+            elif ci % 6 == 3:
+                shares = (("s", 0, 3, 0, N), ("v", 3, 4, 0, N))
             else:
                 shares = (("s", 0, 4, 0, N),)
             for eng, u0, u1, n0, n1 in shares:
@@ -135,8 +145,6 @@ def tile_moe_tk_lin_none_kernel(tc, xT, w, gate, offs, pos1, pos2, pos3, pos4, o
                 e, a = divmod(unit + u, PASSES)
                 b, i = bank_of[e]
                 g = e // GROUP
-                if g not in groups:
-                    gather_group(g)
                 late, ta, tb = groups[g]
                 here = slice((e - g * GROUP) * C, (e - g * GROUP + 1) * C)
                 plane, k = (ta, 4 * a) if a < 4 else (tb, 0)
@@ -150,15 +158,26 @@ def tile_moe_tk_lin_none_kernel(tc, xT, w, gate, offs, pos1, pos2, pos3, pos4, o
                     start=(a == 0),
                     stop=(a == PASSES - 1),
                 )
-                if a == PASSES - 1 and e == BANK_EXPERTS[b][-1]:
-                    first = BANK_EXPERTS[b][0] * C
-                    width = len(BANK_EXPERTS[b]) * C
-                    nc.scalar.copy(y[:, first : first + width], banks[b][:, 0:width])
+
+        def evacuate(b):
+            first = BANK_EXPERTS[b][0] * C
+            width = len(BANK_EXPERTS[b]) * C
+            nc.scalar.copy(y[:, first : first + width], banks[b][:, 0:width])
 
         LAG = 3
+        EVAC_LAG = 5
+        evac_at = {}
+        for b, es in enumerate(BANK_EXPERTS):
+            closed = max(i for i, f in enumerate(firsts) if f <= es[-1] * PASSES + PASSES - 1)
+            evac_at.setdefault(min(closed + LAG + (EVAC_LAG if b < 4 else 0), len(CHUNKS) + LAG - 1), []).append(b)
+        for g in range(n_groups):
+            if g not in region_of:
+                gather_group(g)
         for ci in range(len(CHUNKS) + LAG):
             if ci < len(CHUNKS):
                 prepare(ci)
+            if ci in after:
+                gather_group(after[ci])
             if ci == 20:
                 for t, src in zip(pos_t, (pos1, pos2, pos3, pos4)):
                     nc.sync.dma_start(t[:], src)
@@ -167,6 +186,8 @@ def tile_moe_tk_lin_none_kernel(tc, xT, w, gate, offs, pos1, pos2, pos3, pos4, o
                 nc.sync.dma_start(gate_t[:], gate.rearrange("r p t -> p r t"))
             if ci >= LAG:
                 multiply(ci - LAG)
+            for b in evac_at.get(ci, []):
+                evacuate(b)
 
         prod = xraw_pool.tile([P, 4, T], F32, name="xraw")
         for lo, hi in ((0, 320), (320, 640)):

@@ -16,6 +16,7 @@ U16 = mybir.dt.uint16
 U8 = mybir.dt.uint8
 FP8X4 = mybir.dt.float8_e4m3fn_x4
 MULT = mybir.AluOpType.mult
+ADD = mybir.AluOpType.add
 
 GROUP = 2
 REGIONS = 9
@@ -111,6 +112,8 @@ def tile_moe_tk_lin_none_kernel(tc, xT, w, gate, offs, pos1, pos2, pos3, pos4, o
             src = raw[:, u0:u1, :, n0:n1].rearrange("p u t (c i) -> p u c t i", i=4)
             if eng == "s":
                 nc.scalar.copy(dst, src)
+            elif eng == "g":
+                nc.gpsimd.tensor_scalar(dst, src, 1.0, 0.0, MULT, ADD)
             else:
                 nc.vector.tensor_copy(dst, src)
 
@@ -123,8 +126,8 @@ def tile_moe_tk_lin_none_kernel(tc, xT, w, gate, offs, pos1, pos2, pos3, pos4, o
             grp = ring.tile([P, 4, N, 4], BF16, name=f"wgrp{ci}", align_bytes=64, offset=(ci % REGIONS) * REGION)
             if size < 4:
                 shares = (("s", 0, size, 0, N // 2), ("v", 0, size, N // 2, N))
-            elif ci % 6 == 3:
-                shares = (("s", 0, 3, 0, N), ("v", 3, 4, 0, N))
+            elif ci % 2 == 1:
+                shares = (("s", 0, 3, 0, N), ("g", 3, 4, 0, N))
             else:
                 shares = (("s", 0, 4, 0, N),)
             for eng, u0, u1, n0, n1 in shares:
@@ -190,11 +193,26 @@ def tile_moe_tk_lin_none_kernel(tc, xT, w, gate, offs, pos1, pos2, pos3, pos4, o
                 evacuate(b)
 
         prod = xraw_pool.tile([P, 4, T], F32, name="xraw")
-        for lo, hi in ((0, 320), (320, 640)):
-            for r in range(4):
-                nc.vector.tensor_tensor(
-                    prod[:, r, lo:hi], y[:].indirect(pos_t[r][:, lo // 16 : hi // 16]), gate_t[:, r, lo:hi], MULT
-                )
+        def weigh(r, lo, hi):
+            nc.vector.tensor_tensor(
+                prod[:, r, lo:hi], y[:].indirect(pos_t[r][:, lo // 16 : hi // 16]), gate_t[:, r, lo:hi], MULT
+            )
+
+        def add_pairs(lo, hi):
             nc.vector.tensor_add(half[:, :, lo:hi], prod[:, 0:2, lo:hi], prod[:, 2:4, lo:hi])
+
+        def finish(lo, hi):
             nc.vector.tensor_add(res[:, lo:hi], half[:, 0, lo:hi], half[:, 1, lo:hi])
             nc.sync.dma_start(out[:, lo:hi], res[:, lo:hi])
+
+        CUT = 384
+        for r in range(4):
+            weigh(r, 0, CUT)
+        weigh(0, CUT, T)
+        add_pairs(0, CUT)
+        weigh(1, CUT, T)
+        finish(0, CUT)
+        weigh(2, CUT, T)
+        weigh(3, CUT, T)
+        add_pairs(CUT, T)
+        finish(CUT, T)

@@ -124,12 +124,12 @@ def tile_moe_tk_lin_none_kernel(tc, xT, w, gate, offs, pos1, pos2, pos3, pos4, o
                 raw[:, 0:size].rearrange("p u j n -> p u (j n)"), w_units[:, unit : unit + size, :]
             )
             grp = ring.tile([P, 4, N, 4], BF16, name=f"wgrp{ci}", align_bytes=64, offset=(ci % REGIONS) * REGION)
-            if size < 4:
+            if 1 < size < 4 or ci == len(CHUNKS) - 2:
+                shares = (("s", 0, size, 0, N),)
+            elif size < 4:
                 shares = (("s", 0, size, 0, N // 2), ("v", 0, size, N // 2, N))
-            elif ci % 2 == 1:
-                shares = (("s", 0, 3, 0, N), ("g", 3, 4, 0, N))
             else:
-                shares = (("s", 0, 4, 0, N),)
+                shares = (("s", 0, 3, 0, N), ("g", 3, 4, 0, N))
             for eng, u0, u1, n0, n1 in shares:
                 interleave(eng, grp, raw, u0, u1, n0, n1)
             codes = wq_pool.tile([P, 4 * N], U32, name="wcodes", align_bytes=64)
@@ -186,7 +186,8 @@ def tile_moe_tk_lin_none_kernel(tc, xT, w, gate, offs, pos1, pos2, pos3, pos4, o
                     nc.sync.dma_start(t[:], src)
             if ci == len(CHUNKS) - 1:
                 gate_t = xraw_pool.tile([P, 4, T], F32, name="xraw")
-                nc.sync.dma_start(gate_t[:], gate.rearrange("r p t -> p r t"))
+                for r in range(4):
+                    nc.sync.dma_start(gate_t[:, r, :], gate[r])
             if ci >= LAG:
                 multiply(ci - LAG)
             for b in evac_at.get(ci, []):

from contextlib import ExitStack

import concourse.mybir as mybir

K, T, E, C, N = 2560, 640, 20, 128, 128
SLOTS = E * C
P = 128
PASSES = 5
UNITS = E * PASSES
FLOPS = 2 * SLOTS * K * N

F32 = mybir.dt.float32
BF16 = mybir.dt.bfloat16
U32 = mybir.dt.uint32
U16 = mybir.dt.uint16
U8 = mybir.dt.uint8
FP8X4 = mybir.dt.float8_e4m3fn_x4
MULT = mybir.AluOpType.mult
ADD = mybir.AluOpType.add

GROUP = 2
REGIONS = 9
REGION = 4096
AHEAD = 3
EARLY = 2
CHUNKS = [4] * 24 + [2, 1, 1]
BANK_EXPERTS = [[0, 1, 2, 3], [4, 5, 6, 7], [8, 9, 10, 11], [12, 13, 14, 15], [16, 17, 18], [19]]


def tile_moe_tk_lin_none_kernel(tc, xT, w, gate, offs, pos1, pos2, pos3, pos4, out):
    nc = tc.nc
    with ExitStack() as ctx:
        keep = ctx.enter_context(tc.tile_pool(name="keep", bufs=1))
        xraw_pool = ctx.enter_context(tc.tile_pool(name="xraw", bufs=3))
        xgrp_pool = ctx.enter_context(tc.tile_pool(name="xgrp", bufs=2))
        wraw_pool = ctx.enter_context(tc.tile_pool(name="wraw", bufs=9))
        ring = ctx.enter_context(tc.tile_pool(name="ring", bufs=1))
        wq_pool = ctx.enter_context(tc.tile_pool(name="wq", bufs=10))
        psum = ctx.enter_context(tc.psum_pool(name="psum", bufs=1))

        offs_t = keep.tile([P, SLOTS // 16], U16, name="offs_t")
        nc.sync.dma_start(offs_t[:], offs)
        pos_t = [keep.tile([P, T // 16], U16, name=f"pos_t{r}") for r in range(4)]

        words = [keep.tile([P, T], U32, name=f"words{a}", align_bytes=64) for a in range(PASSES)]
        bytes_a = keep.tile([P, T], U8, name="bytes_a", align_bytes=64)
        bytes_b = keep.tile([P, T], U8, name="bytes_b", align_bytes=64)
        gwords_early = [keep.tile([P, SLOTS], U32, name=f"gwords{a}", align_bytes=64) for a in range(EARLY)]
        y = keep.tile([P, SLOTS], F32, name="y")
        half = keep.tile([P, 2, T], F32, name="half")
        res = keep.tile([P, T], F32, name="res")
        banks = [psum.tile([P, 512], F32, name=f"bank{b}") for b in range(len(BANK_EXPERTS))]

        nc.gpsimd.memset(bytes_a[:], 0)
        nc.gpsimd.memset(bytes_b[:], 0)

        def gather(dst, src, first, count):
            nc.vector.tensor_copy(dst, src[:].indirect(offs_t[:, first // 16 : (first + count) // 16]))

        for a in range(PASSES):
            raw = xraw_pool.tile([P, 4, T], F32, name="xraw")
            nc.sync.dma_start(raw[:], xT[512 * a : 512 * (a + 1), :].rearrange("(p j) t -> p j t", j=4))
            grp = xgrp_pool.tile([P, T, 4], BF16, name="xgrp", align_bytes=64)
            for lo, hi, eng in ((0, 256, "s"), (256, 640, "v")) if a == 0 else ((0, 640, "s"),):
                dst = grp[:, lo:hi, :].rearrange("p (c i) t -> p c t i", i=4)
                src = raw[:, :, lo:hi].rearrange("p t (c i) -> p c t i", i=4)
                if eng == "s":
                    nc.scalar.copy(dst, src)
                else:
                    nc.vector.tensor_copy(dst, src)
            flat = grp[:].rearrange("p t j -> p (t j)")
            plane, k = (bytes_a, 4 * a) if a < 4 else (bytes_b, 0)
            for lo, hi in ((0, 512), (512, 640)):
                nc.vector.quantize_mx(
                    out=words[a][:, lo:hi].bitcast(FP8X4),
                    scales=plane[k:P, lo:hi],
                    in_=flat[:, 4 * lo : 4 * hi],
                )
            if a < EARLY:
                for s in range(0, SLOTS, 480):
                    c = min(480, SLOTS - s)
                    gather(gwords_early[a][:, s : s + c], words[a], s, c)

        w_units = w.rearrange("e (a p j) n -> p (e a) (j n)", a=PASSES, j=4)
        bank_of = {e: (b, i) for b, es in enumerate(BANK_EXPERTS) for i, e in enumerate(es)}
        firsts = [sum(CHUNKS[:i]) for i in range(len(CHUNKS))]
        quantised = {}
        groups = {}
        n_groups = (E + GROUP - 1) // GROUP
        first_use = {g: g * GROUP * PASSES // 4 for g in range(n_groups)}
        after = {first_use[g] - AHEAD: g for g in range(n_groups) if first_use[g] >= AHEAD}
        region_of = {g: c % REGIONS for c, g in after.items()}

        def gather_group(g):
            first = g * GROUP * C
            count = min(GROUP * C, SLOTS - first)
            at = (region_of[g] if g in region_of else REGIONS + g) * REGION
            late = []
            for a in range(EARLY, PASSES):
                t = ring.tile([P, GROUP * C], U32, name=f"late{a}_{g}", align_bytes=64, offset=at)
                at += 4 * GROUP * C
                gather(t[:, 0:count], words[a], first, count)
                late.append(t)
            ta = ring.tile([P, GROUP * C], U8, name=f"gba{g}", align_bytes=64, offset=at)
            gather(ta[:, 0:count], bytes_a, first, count)
            tb = ring.tile([P, GROUP * C], U8, name=f"gbb{g}", align_bytes=64, offset=at + GROUP * C)
            gather(tb[:, 0:count], bytes_b, first, count)
            groups[g] = (late, ta, tb)

        def interleave(eng, grp, raw, u0, u1, n0, n1):
            dst = grp[:, u0:u1, n0:n1, :].rearrange("p u (c i) t -> p u c t i", i=4)
            src = raw[:, u0:u1, :, n0:n1].rearrange("p u t (c i) -> p u c t i", i=4)
            if eng == "s":
                nc.scalar.copy(dst, src)
            elif eng == "g":
                nc.gpsimd.tensor_scalar(dst, src, 1.0, 0.0, MULT, ADD)
            else:
                nc.vector.tensor_copy(dst, src)

        def prepare(ci):
            unit, size = firsts[ci], CHUNKS[ci]
            raw = wraw_pool.tile([P, 4, 4, N], F32, name="wraw")
            nc.sync.dma_start(
                raw[:, 0:size].rearrange("p u j n -> p u (j n)"), w_units[:, unit : unit + size, :]
            )
            grp = ring.tile([P, 4, N, 4], BF16, name=f"wgrp{ci}", align_bytes=64, offset=(ci % REGIONS) * REGION)
            if 1 < size < 4 or ci == len(CHUNKS) - 2:
                shares = (("s", 0, size, 0, N),)
            elif size < 4:
                shares = (("s", 0, size, 0, N // 2), ("v", 0, size, N // 2, N))
            else:
                shares = (("s", 0, 3, 0, N), ("g", 3, 4, 0, N))
            for eng, u0, u1, n0, n1 in shares:
                interleave(eng, grp, raw, u0, u1, n0, n1)
            codes = wq_pool.tile([P, 4 * N], U32, name="wcodes", align_bytes=64)
            scales = wq_pool.tile([P, 4 * N], U8, name="wscales", align_bytes=64)
            nc.vector.quantize_mx(
                out=codes[:, 0 : size * N].bitcast(FP8X4),
                scales=scales[:, 0 : size * N],
                in_=grp[:, 0:size].rearrange("p u n j -> p (u n j)"),
            )
            quantised[ci] = (codes, scales)

        def multiply(ci):
            unit, size = firsts[ci], CHUNKS[ci]
            codes, scales = quantised.pop(ci)
            for u in range(size):
                e, a = divmod(unit + u, PASSES)
                b, i = bank_of[e]
                g = e // GROUP
                late, ta, tb = groups[g]
                here = slice((e - g * GROUP) * C, (e - g * GROUP + 1) * C)
                plane, k = (ta, 4 * a) if a < 4 else (tb, 0)
                rhs = gwords_early[a][:, e * C : (e + 1) * C] if a < EARLY else late[a - EARLY][:, here]
                nc.tensor.matmul_mx(
                    out=banks[b][:, i * C : (i + 1) * C],
                    lhsT=codes[:, u * N : (u + 1) * N].bitcast(FP8X4),
                    lhsT_scale=scales[:, u * N : (u + 1) * N],
                    rhs=rhs.bitcast(FP8X4),
                    rhs_scale=plane[k:P, here],
                    start=(a == 0),
                    stop=(a == PASSES - 1),
                )

        def evacuate(b):
            first = BANK_EXPERTS[b][0] * C
            width = len(BANK_EXPERTS[b]) * C
            nc.scalar.copy(y[:, first : first + width], banks[b][:, 0:width])

        LAG = 3
        EVAC_LAG = 5
        evac_at = {}
        for b, es in enumerate(BANK_EXPERTS):
            closed = max(i for i, f in enumerate(firsts) if f <= es[-1] * PASSES + PASSES - 1)
            evac_at.setdefault(min(closed + LAG + (EVAC_LAG if b < 4 else 0), len(CHUNKS) + LAG - 1), []).append(b)
        for g in range(n_groups):
            if g not in region_of:
                gather_group(g)
        for ci in range(len(CHUNKS) + LAG):
            if ci < len(CHUNKS):
                prepare(ci)
            if ci in after:
                gather_group(after[ci])
            if ci == 20:
                for t, src in zip(pos_t, (pos1, pos2, pos3, pos4)):
                    nc.sync.dma_start(t[:], src)
            if ci == len(CHUNKS) - 1:
                gate_t = xraw_pool.tile([P, 4, T], F32, name="xraw")
                for r in range(4):
                    nc.sync.dma_start(gate_t[:, r, :], gate[r])
            if ci >= LAG:
                multiply(ci - LAG)
            for b in evac_at.get(ci, []):
                evacuate(b)

        prod = xraw_pool.tile([P, 4, T], F32, name="xraw")
        def weigh(r, lo, hi):
            nc.vector.tensor_tensor(
                prod[:, r, lo:hi], y[:].indirect(pos_t[r][:, lo // 16 : hi // 16]), gate_t[:, r, lo:hi], MULT
            )

        def add_pairs(lo, hi):
            nc.vector.tensor_add(half[:, :, lo:hi], prod[:, 0:2, lo:hi], prod[:, 2:4, lo:hi])

        def finish(lo, hi):
            nc.vector.tensor_add(res[:, lo:hi], half[:, 0, lo:hi], half[:, 1, lo:hi])
            nc.sync.dma_start(out[:, lo:hi], res[:, lo:hi])

        CUT = 384
        for r in range(4):
            weigh(r, 0, CUT)
        weigh(0, CUT, T)
        add_pairs(0, CUT)
        weigh(1, CUT, T)
        finish(0, CUT)
        weigh(2, CUT, T)
        weigh(3, CUT, T)
        add_pairs(CUT, T)
        finish(CUT, T)
